import numpy as np, ml_dtypes
CORES = [24,48,72,152,176,200]
N = 6
S, B = 3, 64
NT = N * S
def setup_inputs(rng):
    a = (rng.standard_normal((128, 128), dtype=np.float32) / 12).astype(ml_dtypes.bfloat16)
    return {"x": rng.standard_normal((N, 128, S * B), dtype=np.float32).astype(ml_dtypes.bfloat16), "a": np.broadcast_to(a, (N, 128, 128)).copy(), "at": np.broadcast_to(a.T, (N, 128, 128)).copy()}
def setup_inputs_big(rng):
    d = setup_inputs(rng)
    for k in ("x",): d[k] = (d[k].astype(np.float32) * 1048576.0).astype(d[k].dtype)
    return d
def setup_inputs_small(rng):
    d = setup_inputs(rng)
    for k in ("x",): d[k] = (d[k].astype(np.float32) * (1 / 1048576.0)).astype(d[k].dtype)
    return d
def setup_inputs_apart(rng):
    d = setup_inputs(rng)
    f = (10.0 ** rng.permutation(np.linspace(-1.5, 1.5, N))).astype(np.float32).reshape(N, 1, 1)
    for k in ("x",): d[k] = (d[k].astype(np.float32) * f).astype(d[k].dtype)
    return d
def reference(x, a, at):
    A = a[0].astype(np.float64); X = [x[t // S][:, B * (t % S):B * (t % S) + B].astype(np.float64) for t in range(NT)]
    f = [None] * NT; b = [None] * NT; h = np.zeros((128, B))
    for t in range(NT):
        h = A.T @ h + X[t]; f[t] = h
    h = np.zeros((128, B))
    for t in range(NT - 1, -1, -1):
        h = A.T @ h + X[t]; b[t] = h
    return {"y": np.stack([np.concatenate([f[r * S + s] + b[r * S + s] for s in range(S)], axis=1) for r in range(N)]).astype(ml_dtypes.bfloat16)}

@@ -1,0 +1,313 @@
+from concourse.bass import DstId, RemoteDMATransfer
+from concourse.mybir import AluOpType
+
+N, S, B, D = 6, 3, 64, 128
+POWERS = (1, 2, 3, 4, 5, 6, 10, 11, 12)
+QPOWERS = (1, 2, 4, 8)
+FEED_ENGINES = 8
+FORWARD_ENGINES = 4
+NEV = 36
+
+SCRATCH = {
+    "xs": ("sbuf", [D, S * B], "bfloat16"),
+    "x2": ("sbuf", [D, S * B], "bfloat16"),
+    "pb": ("sbuf", [D, D * len(POWERS)], "bfloat16"),
+    "qb": ("sbuf", [D, D * len(QPOWERS)], "bfloat16"),
+    "ub": ("sbuf", [D, 2 * B], "bfloat16"),
+    "w": ("sbuf", [D, 2 * B], "bfloat16"),
+    "land": ("sbuf", [D, N * B], "bfloat16"),
+    "zs": ("sbuf", [D, 2 * B], "bfloat16"),
+    "ys": ("sbuf", [D, S * B], "bfloat16"),
+    "hbuf": ("sbuf", [D, B], "bfloat16"),
+    "pF": ("psum", [D, 512], "float32"),
+    "pB": ("psum", [D, 512], "float32"),
+    "pwA": ("psum", [D, 512], "float32"),
+    "pwB": ("psum", [D, 512], "float32"),
+    "pZ": ("psum", [D, 512], "float32"),
+    "y0": ("psum", [D, 512], "float32"),
+    "y1": ("psum", [D, 512], "float32"),
+    "y2": ("psum", [D, 512], "float32"),
+}
+SEMAPHORES = ["c%d" % q for q in range(N)] + ["h", "snt"] + ["e%d" % i for i in range(NEV)]
+
+
+def _bits(mask):
+    return [i for i in range(mask.bit_length()) if (mask >> i) & 1]
+
+
+def _mask(bits):
+    return sum(1 << i for i in bits)
+
+
+def _kind(q, r):
+    return "F" if r > q else "B"
+
+
+def _relays(cores, topo):
+    world = range(topo.CORES_PER_HOST * (1 + max(topo.host(c) for c in cores)))
+    used, out_load, in_load, relay = set(cores), {}, {}, {}
+    for q, cq in enumerate(cores):
+        for r, cr in enumerate(cores):
+            if q == r or topo.may_write(cq, cr):
+                continue
+            cands = [h for h in world if h not in used and topo.host(h) == topo.host(cq) and topo.chip(h) == topo.chip(cq)
+                     and topo.may_write(cq, h) and topo.may_write(h, cr)]
+            h = min(cands, key=lambda c: (out_load.get((q, topo.die(c)), 0) + in_load.get((r, topo.die(c)), 0),
+                                          topo.die(c) != topo.die(cq), c))
+            d = topo.die(h)
+            out_load[q, d] = out_load.get((q, d), 0) + 1
+            in_load[r, d] = in_load.get((r, d), 0) + 1
+            used.add(h)
+            relay[q, r] = h
+    return relay
+
+
+def _direct(q, cores, topo):
+    groups = {}
+    for r, cr in enumerate(cores):
+        if r != q and topo.may_write(cores[q], cr):
+            groups.setdefault(_kind(q, r), []).append(r)
+    out = []
+    for j, k in enumerate(sorted(groups)):
+        pool = _bits(topo.mask(cores[q], cores[groups[k][0]]))
+        out.append((k, groups[k], pool[j::len(groups)]))
+    return out
+
+
+def _feeds(q, cores, topo, relay):
+    me = cores[q]
+    jobs = [(relay[q, r], r) for r in range(len(cores)) if (q, r) in relay]
+    near = [j for j in jobs if topo.die(j[0]) == topo.die(me)]
+    far = [j for j in jobs if topo.die(j[0]) != topo.die(me)]
+    order = []
+    while near or far:
+        if near:
+            order.append(near.pop(0))
+        if far:
+            order.append(far.pop(0))
+    first = [e for t in _direct(q, cores, topo) for e in t[2]]
+    allowed = _bits(topo.mask(me, order[0][0]))
+    pool = sorted(([e for e in sorted(first) if e in allowed] + [e for e in allowed if e not in first])[:FEED_ENGINES])
+    return [(h, r, pool[j::len(order)]) for j, (h, r) in enumerate(order)]
+
+
+def _forward_engines(h, dst, topo):
+    pool = _bits(topo.mask(h, dst))
+    return pool[::len(pool) // FORWARD_ENGINES]
+
+
+def _arrival(q, r, cores, topo, relay):
+    if (q, r) in relay:
+        return len(_forward_engines(relay[q, r], cores[r], topo))
+    return [len(e) for k, rs, e in _direct(q, cores, topo) if r in rs][0]
+
+
+def _forward(g, core, T, topo, cores, relay, q, r):
+    fed = [len(e) for h, rr, e in _feeds(q, cores, topo, relay) if h == core][0]
+    eng = _forward_engines(core, cores[r], topo)
+    rid, pid = topo.addr(cores[r], core)
+    g.wait_ge(T.sem.h, fed)
+    g.remote_dma(out_ap=T.land[:, B * q:B * q + B], in_ap=T.hbuf[:], remote_sem=T.sem["c%d" % q], local_sem=T.sem.snt,
+                 pid=pid, routing_id=rid, dma_engine_mask=_mask(eng))
+    g.wait_ge(T.sem.snt, len(eng))
+
+
+def _rank(g, core, T, topo, cores, relay, me):
+    te, ve, sy, sc = g.tensor, g.vector, g.sync, g.scalar
+    add = AluOpType.add
+    nev = [0]
+
+    def ev():
+        nev[0] += 1
+        return [T.sem["e%d" % (nev[0] - 1)], 0]
+
+    def sig(inst, e, k=1):
+        inst.then_inc(e[0], k)
+        e[1] += k
+
+    def wait(queue, e):
+        queue.wait_ge(e[0], e[1])
+
+    pcol = {e: i for i, e in enumerate(POWERS)}
+    qcol = {e: i for i, e in enumerate(QPOWERS)}
+    slot = {"F": 0, "B": 1}
+
+    def X(s):
+        return T.xs[:, B * s:B * s + B]
+
+    def P(lo, hi=None):
+        return T.pb[:, D * pcol[lo]:D * (pcol[hi or lo] + 1)]
+
+    def Q(e):
+        return T.qb[:, D * qcol[e]:D * qcol[e] + D]
+
+    def two(buf, k):
+        return buf[:, B * slot[k]:B * slot[k] + B]
+
+    def expo(kind, k, s):
+        return 3 * k + (s + 1 if kind == "F" else S - s)
+
+    others = [q for q in range(N) if q != me]
+    dist = {q: abs(me - q) - 1 for q in others}
+    early = [q for q in others if (q, me) not in relay]
+    late = sorted((q for q in others if (q, me) in relay), key=lambda q: (0 < q < N - 1, q))
+    gather = {k: [q for q in early if _kind(q, me) == k and dist[q] > 0] for k in ("F", "B")}
+    need = [expo(_kind(q, me), dist[q], s) for q in late for s in range(S)] + [3 * dist[q] for k in gather for q in gather[k]]
+    far_powers = max(need) > 6
+
+    ex, ea, et = ev(), ev(), ev()
+    sig(sy.dma_start(T.xs[:], T.x[:]), ex, 16)
+    sig(sc.dma_start(P(1), T.a[:]), ea, 16)
+    sig(sc.dma_start(Q(1), T.at[:]), et, 16)
+
+    head, tail = {"F": 0, "B": 2}, {"F": 2, "B": 0}
+    bank = {"F": T.pF, "B": T.pB}
+    send = [k for k in ("F", "B") if any(_kind(me, r) == k for r in others)]
+    rest = [k for k in ("F", "B") if k not in send]
+    em1, eu, em2, efb = {}, {}, {}, ev()
+    wait(te, ex)
+    wait(te, ea)
+    wait(ve, ex)
+    for k in send + rest:
+        em1[k] = ev()
+        sig(te.matmul(bank[k][:, 0:B], P(1), X(head[k]), True, True), em1[k])
+    for k in send:
+        eu[k] = ev()
+        wait(ve, em1[k])
+        sig(ve.tensor_tensor(two(T.ub, k), bank[k][:, 0:B], X(1), add), eu[k])
+    for k in send:
+        em2[k] = ev()
+        wait(te, eu[k])
+        sig(te.matmul(bank[k][:, B:2 * B], P(1), two(T.ub, k), True, True), em2[k])
+    for k in send:
+        wait(ve, em2[k])
+        sig(ve.tensor_tensor(two(T.w, k), bank[k][:, B:2 * B], X(tail[k]), add), efb)
+    for k in rest:
+        eu[k] = ev()
+        wait(ve, em1[k])
+        sig(ve.tensor_tensor(two(T.ub, k), bank[k][:, 0:B], X(1), add), eu[k])
+
+    wait(g, efb)
+    sent, feed, direct = 0, [], []
+    for h, r, eng in _feeds(me, cores, topo, relay):
+        rid, pid = topo.addr(h, core)
+        feed.append(RemoteDMATransfer(dst_ids=[DstId(rid=rid, pnc=pid)], dma_engine_mask=_mask(eng), remote_sem=T.sem.h,
+                                      srcs=[two(T.w, _kind(me, r))], dsts=[T.hbuf[:]]))
+        sent += len(eng)
+    g.remote_dma_fused(feed, local_sem=T.sem.snt)
+    for k, rs, eng in _direct(me, cores, topo):
+        ids = [topo.addr(cores[r], core) for r in rs]
+        direct.append(RemoteDMATransfer(dst_ids=[DstId(rid=rid, pnc=pid) for rid, pid in ids], dma_engine_mask=_mask(eng),
+                                        remote_sem=T.sem["c%d" % me], srcs=[two(T.w, k)],
+                                        dsts=[T.land[:, B * me:B * me + B] for r in rs]))
+        sent += len(eng)
+    g.remote_dma_fused(direct, local_sem=T.sem.snt)
+    g.wait_ge(T.sem.snt, sent)
+
+    Y = [T.y0, T.y1, T.y2]
+    ey = [ev() for s in range(S)]
+    started = [False] * S
+
+    def acc(s, e, rhs, stop=False):
+        sig(te.matmul(Y[s][:, 0:B], P(e), rhs, not started[s], stop), ey[s])
+        started[s] = True
+
+    def stage(out, lhsT, rhs):
+        e = ev()
+        sig(te.matmul(out, lhsT, rhs, True, True), e)
+        return e
+
+    def keep(dst, src, made):
+        e = ev()
+        wait(ve, made)
+        sig(ve.tensor_copy(dst, src), e)
+        return e
+
+    wait(te, et)
+    mq = stage(T.pwB[:, 0:D], P(1), Q(1))
+    mp = stage(T.pwA[:, 0:D], Q(1), P(1))
+    for k in ("F", "B"):
+        wait(te, eu[k])
+    acc(0, 1, two(T.ub, "B"))
+    acc(1, 1, X(0))
+    acc(1, 1, X(2))
+    acc(2, 1, two(T.ub, "F"))
+    kq = keep(Q(2), T.pwB[:, 0:D], mq)
+    kp = keep(P(2), T.pwA[:, 0:D], mp)
+    wait(te, kq)
+    wait(te, kp)
+    if far_powers:
+        mq = stage(T.pwB[:, 0:D], P(2), Q(2))
+        mp = stage(T.pwA[:, 0:2 * D], Q(2), P(1, 2))
+        kq = keep(Q(4), T.pwB[:, 0:D], mq)
+        kp = keep(P(3, 4), T.pwA[:, 0:2 * D], mp)
+        wait(te, kq)
+        wait(te, kp)
+        mq = stage(T.pwB[:, 0:D], P(4), Q(4))
+        mp = stage(T.pwA[:, 0:2 * D], Q(4), P(1, 2))
+        kq = keep(Q(8), T.pwB[:, 0:D], mq)
+        kp = keep(P(5, 6), T.pwA[:, 0:2 * D], mp)
+        wait(te, kq)
+        mp2 = stage(T.pwB[:, 0:3 * D], Q(8), P(2, 4))
+        kp2 = keep(P(10, 12), T.pwB[:, 0:3 * D], mp2)
+        wait(te, kp)
+        wait(te, kp2)
+    else:
+        mp = stage(T.pwA[:, 0:2 * D], Q(2), P(1, 2))
+        kp = keep(P(3, 4), T.pwA[:, 0:2 * D], mp)
+        wait(te, kp)
+        mp = stage(T.pwB[:, 0:2 * D], Q(2), P(3, 4))
+        kp = keep(P(5, 6), T.pwB[:, 0:2 * D], mp)
+        wait(te, kp)
+    e2x = ev()
+    sig(ve.tensor_tensor(T.x2[:], T.xs[:], T.xs[:], add), e2x)
+
+    def src(q):
+        return T.land[:, B * q:B * q + B]
+
+    def arrived(q):
+        te.wait_ge(T.sem["c%d" % q], _arrival(q, me, cores, topo, relay))
+
+    for q in early:
+        arrived(q)
+    kinds = [k for k in ("F", "B") if gather[k]]
+    emz = ev()
+    for k in kinds:
+        for i, q in enumerate(gather[k]):
+            sig(te.matmul(two(T.pZ, k), P(3 * dist[q]), src(q), i == 0, i == len(gather[k]) - 1), emz)
+    for q in early:
+        if dist[q] == 0:
+            for s in range(S):
+                acc(s, expo(_kind(q, me), 0, s), src(q))
+    lo, hi = B * slot[kinds[0]], B * slot[kinds[-1]] + B
+    ez = keep(T.zs[:, lo:hi], T.pZ[:, lo:hi], emz)
+    wait(te, ez)
+    for k in kinds:
+        for s in range(S):
+            acc(s, expo(k, 0, s), two(T.zs, k))
+
+    for q in late:
+        arrived(q)
+        for s in range(S):
+            acc(s, expo(_kind(q, me), dist[q], s), src(q), q == late[-1])
+
+    eout, est = ev(), ev()
+    wait(ve, e2x)
+    for s in range(S):
+        wait(ve, ey[s])
+        sig(ve.tensor_tensor(T.ys[:, B * s:B * s + B], Y[s][:, 0:B], T.x2[:, B * s:B * s + B], add), eout)
+    wait(sy, eout)
+    sig(sy.dma_start(T.y[:], T.ys[:]), est, 16)
+    wait(sy, est)
+
+
+def rank_program(g, core, T, topo):
+    cores = list(T.cores)
+    relay = _relays(cores, topo)
+    for (q, r), h in relay.items():
+        if h == core:
+            _forward(g, core, T, topo, cores, relay, q, r)
+            return
+    me = T.rank_of(core)
+    if me is not None:
+        _rank(g, core, T, topo, cores, relay, me)

@@ -6,7 +6,7 @@ POWERS = (1, 2, 3, 4, 5, 6, 10, 11, 12)
 QPOWERS = (1, 2, 4, 8)
 FEED_ENGINES = 8
 FORWARD_ENGINES = 4
-NEV = 36
+NEV = 40
 
 SCRATCH = {
     "xs": ("sbuf", [D, S * B], "bfloat16"),
@@ -15,7 +15,9 @@ SCRATCH = {
     "qb": ("sbuf", [D, D * len(QPOWERS)], "bfloat16"),
     "ub": ("sbuf", [D, 2 * B], "bfloat16"),
     "w": ("sbuf", [D, 2 * B], "bfloat16"),
+    "w2": ("sbuf", [D, B], "bfloat16"),
     "land": ("sbuf", [D, N * B], "bfloat16"),
+    "land2": ("sbuf", [D, N * B], "bfloat16"),
     "zs": ("sbuf", [D, 2 * B], "bfloat16"),
     "ys": ("sbuf", [D, S * B], "bfloat16"),
     "hbuf": ("sbuf", [D, B], "bfloat16"),
@@ -28,7 +30,7 @@ SCRATCH = {
     "y1": ("psum", [D, 512], "float32"),
     "y2": ("psum", [D, 512], "float32"),
 }
-SEMAPHORES = ["c%d" % q for q in range(N)] + ["h", "snt"] + ["e%d" % i for i in range(NEV)]
+SEMAPHORES = ["c%d" % q for q in range(N)] + ["t%d" % q for q in range(N)] + ["h", "snt"] + ["e%d" % i for i in range(NEV)]
 
 
 def _bits(mask):
@@ -62,15 +64,23 @@ def _relays(cores, topo):
     return relay
 
 
+def _split(q, cores, topo):
+    return max((r for r in range(len(cores)) if r != q and topo.may_write(cores[q], cores[r])),
+               key=lambda r: (abs(r - q), -r))
+
+
 def _direct(q, cores, topo):
     groups = {}
     for r, cr in enumerate(cores):
         if r != q and topo.may_write(cores[q], cr):
-            groups.setdefault(_kind(q, r), []).append(r)
+            groups.setdefault((_kind(q, r), r == _split(q, cores, topo)), []).append(r)
+    stride = 1
+    while stride < len(groups):
+        stride *= 2
     out = []
     for j, k in enumerate(sorted(groups)):
         pool = _bits(topo.mask(cores[q], cores[groups[k][0]]))
-        out.append((k, groups[k], pool[j::len(groups)]))
+        out.append((k, groups[k], pool[j::stride]))
     return out
 
 
@@ -182,23 +192,35 @@ def _rank(g, core, T, topo, cores, relay, me):
     for k in send:
         wait(ve, em2[k])
         sig(ve.tensor_tensor(two(T.w, k), bank[k][:, B:2 * B], X(tail[k]), add), efb)
+
+    sp = _split(me, cores, topo)
+    ksp = _kind(me, sp)
+    emu = ev()
+    sig(ve.tensor_copy(T.w2[:], bank[ksp][:, B:2 * B]), emu)
     for k in rest:
         eu[k] = ev()
         wait(ve, em1[k])
         sig(ve.tensor_tensor(two(T.ub, k), bank[k][:, 0:B], X(1), add), eu[k])
 
-    wait(g, efb)
     sent, feed, direct = 0, [], []
+    wait(g, ex)
+    eng = _bits(topo.mask(core, cores[sp]))
+    rid, pid = topo.addr(cores[sp], core)
+    g.remote_dma(out_ap=T.land2[:, B * me:B * me + B], in_ap=X(tail[ksp]), remote_sem=T.sem["t%d" % me],
+                 local_sem=T.sem.snt, pid=pid, routing_id=rid, dma_engine_mask=_mask(eng))
+    sent += len(eng)
+    wait(g, efb)
     for h, r, eng in _feeds(me, cores, topo, relay):
         rid, pid = topo.addr(h, core)
         feed.append(RemoteDMATransfer(dst_ids=[DstId(rid=rid, pnc=pid)], dma_engine_mask=_mask(eng), remote_sem=T.sem.h,
                                       srcs=[two(T.w, _kind(me, r))], dsts=[T.hbuf[:]]))
         sent += len(eng)
     g.remote_dma_fused(feed, local_sem=T.sem.snt)
-    for k, rs, eng in _direct(me, cores, topo):
+    wait(g, emu)
+    for (k, parted), rs, eng in _direct(me, cores, topo):
         ids = [topo.addr(cores[r], core) for r in rs]
         direct.append(RemoteDMATransfer(dst_ids=[DstId(rid=rid, pnc=pid) for rid, pid in ids], dma_engine_mask=_mask(eng),
-                                        remote_sem=T.sem["c%d" % me], srcs=[two(T.w, k)],
+                                        remote_sem=T.sem["c%d" % me], srcs=[T.w2[:] if parted else two(T.w, k)],
                                         dsts=[T.land[:, B * me:B * me + B] for r in rs]))
         sent += len(eng)
     g.remote_dma_fused(direct, local_sem=T.sem.snt)
@@ -265,20 +287,29 @@ def _rank(g, core, T, topo, cores, relay, me):
     def src(q):
         return T.land[:, B * q:B * q + B]
 
+    def parts(q):
+        if _split(q, cores, topo) != me:
+            return [src(q)]
+        return [T.land2[:, B * q:B * q + B], src(q)]
+
     def arrived(q):
         te.wait_ge(T.sem["c%d" % q], _arrival(q, me, cores, topo, relay))
 
     for q in early:
+        if _split(q, cores, topo) == me:
+            te.wait_ge(T.sem["t%d" % q], len(_bits(topo.mask(cores[q], core))))
         arrived(q)
     kinds = [k for k in ("F", "B") if gather[k]]
     emz = ev()
     for k in kinds:
-        for i, q in enumerate(gather[k]):
-            sig(te.matmul(two(T.pZ, k), P(3 * dist[q]), src(q), i == 0, i == len(gather[k]) - 1), emz)
+        jobs = [(q, ap) for q in gather[k] for ap in parts(q)]
+        for i, (q, ap) in enumerate(jobs):
+            sig(te.matmul(two(T.pZ, k), P(3 * dist[q]), ap, i == 0, i == len(jobs) - 1), emz)
     for q in early:
         if dist[q] == 0:
-            for s in range(S):
-                acc(s, expo(_kind(q, me), 0, s), src(q))
+            for ap in parts(q):
+                for s in range(S):
+                    acc(s, expo(_kind(q, me), 0, s), ap)
     lo, hi = B * slot[kinds[0]], B * slot[kinds[-1]] + B
     ez = keep(T.zs[:, lo:hi], T.pZ[:, lo:hi], emz)
     wait(te, ez)

from concourse.bass import DstId, RemoteDMATransfer
from concourse.mybir import AluOpType

N, S, B, D = 6, 3, 64, 128
POWERS = (1, 2, 3, 4, 5, 6, 10, 11, 12)
QPOWERS = (1, 2, 4, 8)
FEED_ENGINES = 8
FORWARD_ENGINES = 4
NEV = 40

SCRATCH = {
    "xs": ("sbuf", [D, S * B], "bfloat16"),
    "x2": ("sbuf", [D, S * B], "bfloat16"),
    "pb": ("sbuf", [D, D * len(POWERS)], "bfloat16"),
    "qb": ("sbuf", [D, D * len(QPOWERS)], "bfloat16"),
    "ub": ("sbuf", [D, 2 * B], "bfloat16"),
    "w": ("sbuf", [D, 2 * B], "bfloat16"),
    "w2": ("sbuf", [D, B], "bfloat16"),
    "land": ("sbuf", [D, N * B], "bfloat16"),
    "land2": ("sbuf", [D, N * B], "bfloat16"),
    "zs": ("sbuf", [D, 2 * B], "bfloat16"),
    "ys": ("sbuf", [D, S * B], "bfloat16"),
    "hbuf": ("sbuf", [D, B], "bfloat16"),
    "pF": ("psum", [D, 512], "float32"),
    "pB": ("psum", [D, 512], "float32"),
    "pwA": ("psum", [D, 512], "float32"),
    "pwB": ("psum", [D, 512], "float32"),
    "pZ": ("psum", [D, 512], "float32"),
    "y0": ("psum", [D, 512], "float32"),
    "y1": ("psum", [D, 512], "float32"),
    "y2": ("psum", [D, 512], "float32"),
}
SEMAPHORES = ["c%d" % q for q in range(N)] + ["t%d" % q for q in range(N)] + ["h", "snt"] + ["e%d" % i for i in range(NEV)]


def _bits(mask):
    return [i for i in range(mask.bit_length()) if (mask >> i) & 1]


def _mask(bits):
    return sum(1 << i for i in bits)


def _kind(q, r):
    return "F" if r > q else "B"


def _relays(cores, topo):
    world = range(topo.CORES_PER_HOST * (1 + max(topo.host(c) for c in cores)))
    used, out_load, in_load, relay = set(cores), {}, {}, {}
    for q, cq in enumerate(cores):
        for r, cr in enumerate(cores):
            if q == r or topo.may_write(cq, cr):
                continue
            cands = [h for h in world if h not in used and topo.host(h) == topo.host(cq) and topo.chip(h) == topo.chip(cq)
                     and topo.may_write(cq, h) and topo.may_write(h, cr)]
            h = min(cands, key=lambda c: (out_load.get((q, topo.die(c)), 0) + in_load.get((r, topo.die(c)), 0),
                                          topo.die(c) != topo.die(cq), c))
            d = topo.die(h)
            out_load[q, d] = out_load.get((q, d), 0) + 1
            in_load[r, d] = in_load.get((r, d), 0) + 1
            used.add(h)
            relay[q, r] = h
    return relay


def _split(q, cores, topo):
    return max((r for r in range(len(cores)) if r != q and topo.may_write(cores[q], cores[r])),
               key=lambda r: (abs(r - q), -r))


def _direct(q, cores, topo):
    groups = {}
    for r, cr in enumerate(cores):
        if r != q and topo.may_write(cores[q], cr):
            groups.setdefault((_kind(q, r), r == _split(q, cores, topo)), []).append(r)
    stride = 1
    while stride < len(groups):
        stride *= 2
    out = []
    for j, k in enumerate(sorted(groups)):
        pool = _bits(topo.mask(cores[q], cores[groups[k][0]]))
        out.append((k, groups[k], pool[j::stride]))
    return out


def _feeds(q, cores, topo, relay):
    me = cores[q]
    jobs = [(relay[q, r], r) for r in range(len(cores)) if (q, r) in relay]
    near = [j for j in jobs if topo.die(j[0]) == topo.die(me)]
    far = [j for j in jobs if topo.die(j[0]) != topo.die(me)]
    order = []
    while near or far:
        if near:
            order.append(near.pop(0))
        if far:
            order.append(far.pop(0))
    first = [e for t in _direct(q, cores, topo) for e in t[2]]
    allowed = _bits(topo.mask(me, order[0][0]))
    pool = sorted(([e for e in sorted(first) if e in allowed] + [e for e in allowed if e not in first])[:FEED_ENGINES])
    return [(h, r, pool[j::len(order)]) for j, (h, r) in enumerate(order)]


def _forward_engines(h, dst, topo):
    pool = _bits(topo.mask(h, dst))
    return pool[::len(pool) // FORWARD_ENGINES]


def _arrival(q, r, cores, topo, relay):
    if (q, r) in relay:
        return len(_forward_engines(relay[q, r], cores[r], topo))
    return [len(e) for k, rs, e in _direct(q, cores, topo) if r in rs][0]


def _forward(g, core, T, topo, cores, relay, q, r):
    fed = [len(e) for h, rr, e in _feeds(q, cores, topo, relay) if h == core][0]
    eng = _forward_engines(core, cores[r], topo)
    rid, pid = topo.addr(cores[r], core)
    g.wait_ge(T.sem.h, fed)
    g.remote_dma(out_ap=T.land[:, B * q:B * q + B], in_ap=T.hbuf[:], remote_sem=T.sem["c%d" % q], local_sem=T.sem.snt,
                 pid=pid, routing_id=rid, dma_engine_mask=_mask(eng))
    g.wait_ge(T.sem.snt, len(eng))


def _rank(g, core, T, topo, cores, relay, me):
    te, ve, sy, sc = g.tensor, g.vector, g.sync, g.scalar
    add = AluOpType.add
    nev = [0]

    def ev():
        nev[0] += 1
        return [T.sem["e%d" % (nev[0] - 1)], 0]

    def sig(inst, e, k=1):
        inst.then_inc(e[0], k)
        e[1] += k

    def wait(queue, e):
        queue.wait_ge(e[0], e[1])

    pcol = {e: i for i, e in enumerate(POWERS)}
    qcol = {e: i for i, e in enumerate(QPOWERS)}
    slot = {"F": 0, "B": 1}

    def X(s):
        return T.xs[:, B * s:B * s + B]

    def P(lo, hi=None):
        return T.pb[:, D * pcol[lo]:D * (pcol[hi or lo] + 1)]

    def Q(e):
        return T.qb[:, D * qcol[e]:D * qcol[e] + D]

    def two(buf, k):
        return buf[:, B * slot[k]:B * slot[k] + B]

    def expo(kind, k, s):
        return 3 * k + (s + 1 if kind == "F" else S - s)

    others = [q for q in range(N) if q != me]
    dist = {q: abs(me - q) - 1 for q in others}
    early = [q for q in others if (q, me) not in relay]
    late = sorted((q for q in others if (q, me) in relay), key=lambda q: (0 < q < N - 1, q))
    gather = {k: [q for q in early if _kind(q, me) == k and dist[q] > 0] for k in ("F", "B")}
    need = [expo(_kind(q, me), dist[q], s) for q in late for s in range(S)] + [3 * dist[q] for k in gather for q in gather[k]]
    far_powers = max(need) > 6

    ex, ea, et = ev(), ev(), ev()
    sig(sy.dma_start(T.xs[:], T.x[:]), ex, 16)
    sig(sc.dma_start(P(1), T.a[:]), ea, 16)
    sig(sc.dma_start(Q(1), T.at[:]), et, 16)

    head, tail = {"F": 0, "B": 2}, {"F": 2, "B": 0}
    bank = {"F": T.pF, "B": T.pB}
    send = [k for k in ("F", "B") if any(_kind(me, r) == k for r in others)]
    rest = [k for k in ("F", "B") if k not in send]
    em1, eu, em2, efb = {}, {}, {}, ev()
    wait(te, ex)
    wait(te, ea)
    wait(ve, ex)
    for k in send + rest:
        em1[k] = ev()
        sig(te.matmul(bank[k][:, 0:B], P(1), X(head[k]), True, True), em1[k])
    for k in send:
        eu[k] = ev()
        wait(ve, em1[k])
        sig(ve.tensor_tensor(two(T.ub, k), bank[k][:, 0:B], X(1), add), eu[k])
    for k in send:
        em2[k] = ev()
        wait(te, eu[k])
        sig(te.matmul(bank[k][:, B:2 * B], P(1), two(T.ub, k), True, True), em2[k])
    for k in send:
        wait(ve, em2[k])
        sig(ve.tensor_tensor(two(T.w, k), bank[k][:, B:2 * B], X(tail[k]), add), efb)

    sp = _split(me, cores, topo)
    ksp = _kind(me, sp)
    emu = ev()
    sig(ve.tensor_copy(T.w2[:], bank[ksp][:, B:2 * B]), emu)
    for k in rest:
        eu[k] = ev()
        wait(ve, em1[k])
        sig(ve.tensor_tensor(two(T.ub, k), bank[k][:, 0:B], X(1), add), eu[k])

    sent, feed, direct = 0, [], []
    wait(g, ex)
    eng = _bits(topo.mask(core, cores[sp]))
    rid, pid = topo.addr(cores[sp], core)
    g.remote_dma(out_ap=T.land2[:, B * me:B * me + B], in_ap=X(tail[ksp]), remote_sem=T.sem["t%d" % me],
                 local_sem=T.sem.snt, pid=pid, routing_id=rid, dma_engine_mask=_mask(eng))
    sent += len(eng)
    wait(g, efb)
    for h, r, eng in _feeds(me, cores, topo, relay):
        rid, pid = topo.addr(h, core)
        feed.append(RemoteDMATransfer(dst_ids=[DstId(rid=rid, pnc=pid)], dma_engine_mask=_mask(eng), remote_sem=T.sem.h,
                                      srcs=[two(T.w, _kind(me, r))], dsts=[T.hbuf[:]]))
        sent += len(eng)
    g.remote_dma_fused(feed, local_sem=T.sem.snt)
    wait(g, emu)
    for (k, parted), rs, eng in _direct(me, cores, topo):
        ids = [topo.addr(cores[r], core) for r in rs]
        direct.append(RemoteDMATransfer(dst_ids=[DstId(rid=rid, pnc=pid) for rid, pid in ids], dma_engine_mask=_mask(eng),
                                        remote_sem=T.sem["c%d" % me], srcs=[T.w2[:] if parted else two(T.w, k)],
                                        dsts=[T.land[:, B * me:B * me + B] for r in rs]))
        sent += len(eng)
    g.remote_dma_fused(direct, local_sem=T.sem.snt)
    g.wait_ge(T.sem.snt, sent)

    Y = [T.y0, T.y1, T.y2]
    ey = [ev() for s in range(S)]
    started = [False] * S

    def acc(s, e, rhs, stop=False):
        sig(te.matmul(Y[s][:, 0:B], P(e), rhs, not started[s], stop), ey[s])
        started[s] = True

    def stage(out, lhsT, rhs):
        e = ev()
        sig(te.matmul(out, lhsT, rhs, True, True), e)
        return e

    def keep(dst, src, made):
        e = ev()
        wait(ve, made)
        sig(ve.tensor_copy(dst, src), e)
        return e

    wait(te, et)
    mq = stage(T.pwB[:, 0:D], P(1), Q(1))
    mp = stage(T.pwA[:, 0:D], Q(1), P(1))
    for k in ("F", "B"):
        wait(te, eu[k])
    acc(0, 1, two(T.ub, "B"))
    acc(1, 1, X(0))
    acc(1, 1, X(2))
    acc(2, 1, two(T.ub, "F"))
    kq = keep(Q(2), T.pwB[:, 0:D], mq)
    kp = keep(P(2), T.pwA[:, 0:D], mp)
    wait(te, kq)
    wait(te, kp)
    if far_powers:
        mq = stage(T.pwB[:, 0:D], P(2), Q(2))
        mp = stage(T.pwA[:, 0:2 * D], Q(2), P(1, 2))
        kq = keep(Q(4), T.pwB[:, 0:D], mq)
        kp = keep(P(3, 4), T.pwA[:, 0:2 * D], mp)
        wait(te, kq)
        wait(te, kp)
        mq = stage(T.pwB[:, 0:D], P(4), Q(4))
        mp = stage(T.pwA[:, 0:2 * D], Q(4), P(1, 2))
        kq = keep(Q(8), T.pwB[:, 0:D], mq)
        kp = keep(P(5, 6), T.pwA[:, 0:2 * D], mp)
        wait(te, kq)
        mp2 = stage(T.pwB[:, 0:3 * D], Q(8), P(2, 4))
        kp2 = keep(P(10, 12), T.pwB[:, 0:3 * D], mp2)
        wait(te, kp)
        wait(te, kp2)
    else:
        mp = stage(T.pwA[:, 0:2 * D], Q(2), P(1, 2))
        kp = keep(P(3, 4), T.pwA[:, 0:2 * D], mp)
        wait(te, kp)
        mp = stage(T.pwB[:, 0:2 * D], Q(2), P(3, 4))
        kp = keep(P(5, 6), T.pwB[:, 0:2 * D], mp)
        wait(te, kp)
    e2x = ev()
    sig(ve.tensor_tensor(T.x2[:], T.xs[:], T.xs[:], add), e2x)

    def src(q):
        return T.land[:, B * q:B * q + B]

    def parts(q):
        if _split(q, cores, topo) != me:
            return [src(q)]
        return [T.land2[:, B * q:B * q + B], src(q)]

    def arrived(q):
        te.wait_ge(T.sem["c%d" % q], _arrival(q, me, cores, topo, relay))

    for q in early:
        if _split(q, cores, topo) == me:
            te.wait_ge(T.sem["t%d" % q], len(_bits(topo.mask(cores[q], core))))
        arrived(q)
    kinds = [k for k in ("F", "B") if gather[k]]
    emz = ev()
    for k in kinds:
        jobs = [(q, ap) for q in gather[k] for ap in parts(q)]
        for i, (q, ap) in enumerate(jobs):
            sig(te.matmul(two(T.pZ, k), P(3 * dist[q]), ap, i == 0, i == len(jobs) - 1), emz)
    for q in early:
        if dist[q] == 0:
            for ap in parts(q):
                for s in range(S):
                    acc(s, expo(_kind(q, me), 0, s), ap)
    lo, hi = B * slot[kinds[0]], B * slot[kinds[-1]] + B
    ez = keep(T.zs[:, lo:hi], T.pZ[:, lo:hi], emz)
    wait(te, ez)
    for k in kinds:
        for s in range(S):
            acc(s, expo(k, 0, s), two(T.zs, k))

    for q in late:
        arrived(q)
        for s in range(S):
            acc(s, expo(_kind(q, me), dist[q], s), src(q), q == late[-1])

    eout, est = ev(), ev()
    wait(ve, e2x)
    for s in range(S):
        wait(ve, ey[s])
        sig(ve.tensor_tensor(T.ys[:, B * s:B * s + B], Y[s][:, 0:B], T.x2[:, B * s:B * s + B], add), eout)
    wait(sy, eout)
    sig(sy.dma_start(T.y[:], T.ys[:]), est, 16)
    wait(sy, est)


def rank_program(g, core, T, topo):
    cores = list(T.cores)
    relay = _relays(cores, topo)
    for (q, r), h in relay.items():
        if h == core:
            _forward(g, core, T, topo, cores, relay, q, r)
            return
    me = T.rank_of(core)
    if me is not None:
        _rank(g, core, T, topo, cores, relay, me)
